import numpy as np
import ml_dtypes


def mxq(x, axis, fmt="e4m3"):
    dtype, down = {"e4m3": (ml_dtypes.float8_e4m3fn, 7), "e5m2": (ml_dtypes.float8_e5m2, 14)}[fmt]
    v = np.moveaxis(np.asarray(x, np.float32).astype(ml_dtypes.bfloat16).astype(np.float64), axis, -1)
    blocks = v.reshape(v.shape[:-1] + (-1, 32))
    amax = np.abs(blocks).max(-1, keepdims=True)
    byte = np.maximum(np.where(amax > 0, np.frexp(amax)[1] - 1 + 127, 0) - down, 1)
    scale = np.exp2(byte - 127.0)
    codes = (blocks / scale).astype(np.float32).astype(dtype).astype(np.float64)
    return np.moveaxis((codes * scale).reshape(v.shape), -1, axis)


WIDE = False


def mx_kscale(k):
    if not WIDE:
        return np.ones(k)
    levels = np.array([10, -10, 5, -5, 0])
    if k % 512:
        return np.exp2(np.random.permutation(np.resize(levels, k // 32))).repeat(32)
    a = np.empty((k // 512, 16))
    for p in range(k // 512):
        a[p, :8] = np.random.permutation(np.resize(levels, 8))
        for g in range(8):
            far = levels[np.abs(levels - a[p, g]) >= 10]
            a[p, g + 8] = far[np.random.randint(len(far))]
    return np.exp2(a.ravel()).repeat(32)


def f64(x):
    return np.asarray(x).astype(np.float64)


def striped(idx):
    return np.tile(idx.reshape(-1, 16).T, (8, 1)).astype(np.uint16)


def unstriped(offs):
    return offs[:16].T.reshape(-1).astype(np.int64)


E2M1 = np.array([0.0, 0.5, 1.0, 1.5, 2.0, 3.0, 4.0, 6.0, -0.0, -0.5, -1.0, -1.5, -2.0, -3.0, -4.0, -6.0])


def pack_weight(w, fmt):
    k, n = w.shape
    w = f64(np.asarray(w, np.float32).astype(ml_dtypes.bfloat16)).reshape(k // 32, 32, n)
    amax = np.abs(w).max(1)
    if fmt == "e4m3":
        byte = np.frexp(amax)[1] - 1 + 127 - 7
    else:
        mant, ex = np.frexp(amax / 6.0)
        byte = np.where(mant > 0.5, ex, ex - 1) + 127
    byte = np.clip(np.where(amax > 0, byte, 1), 1, 254)
    scaled = (w * np.exp2(127.0 - byte)[:, None, :]).reshape(k, n).astype(np.float32)
    by_word = np.ascontiguousarray(scaled.reshape(k // 512, 128, 4, n).transpose(0, 1, 3, 2))
    if fmt == "e4m3":
        words = by_word.astype(ml_dtypes.float8_e4m3fn).view(np.uint8)
    else:
        c = by_word.astype(ml_dtypes.float4_e2m1fn).view(np.uint8) & 0xF
        words = (c[..., 0::2] | (c[..., 1::2] << 4)).reshape(k // 512, 128, 2 * n)
    return np.ascontiguousarray(words), np.ascontiguousarray(byte.astype(np.uint8).reshape(k // 512, 16, n))


def unpack_weight(words, scales, fmt):
    g, _, n = scales.shape
    words = np.ascontiguousarray(words).reshape(g, 128, n, -1)
    if fmt == "e4m3":
        vals = words.view(ml_dtypes.float8_e4m3fn).astype(np.float64)
    else:
        nib = np.empty((g, 128, n, 4), np.uint8)
        nib[..., 0::2] = words & 0xF
        nib[..., 1::2] = words >> 4
        vals = E2M1[nib]
    vals = vals * np.repeat(np.exp2(scales.astype(np.float64) - 127.0), 8, axis=1)[..., None]
    return vals.transpose(0, 1, 3, 2).reshape(g * 512, n)


def gelu(v):
    return 0.5 * v * (1.0 + np.tanh(np.sqrt(2.0 / np.pi) * (v + 0.044715 * v**3)))


K, H, N, T, S, P = 1024, 1024, 384, 4096, 1024, 512

def setup_inputs():
    n = np.random.standard_normal
    s = mx_kscale(K)[:, None]
    u = mx_kscale(H)[:, None]
    tab_words, tab_scales = pack_weight(n((K, T)) * s, "e4m3")
    w4_words, w4_scales = pack_weight(n((K, H)) / np.sqrt(K) / s, "e2m1")
    w8_words, w8_scales = pack_weight(n((H, N)) / np.sqrt(H) / u, "e4m3")
    return {
        "tab_words": tab_words, "tab_scales": tab_scales,
        "offs": striped(np.random.permutation(T)[:S]),
        "pos1": striped(np.random.permutation(S)[:P]),
        "pos2": striped(np.random.permutation(S)[:P]),
        "w1": (n((K, H)) / np.sqrt(K) / s).astype(np.float32),
        "w4_words": w4_words, "w4_scales": w4_scales,
        "gain": (np.exp(0.3 * n(H)) * u[:, 0]).astype(np.float32),
        "solid": np.exp(0.4 * n(H)).astype(np.float32),
        "wl": (n((H, N)) / np.sqrt(H) / u).astype(np.float32),
        "w8_words": w8_words, "w8_scales": w8_scales,
        "fin": np.exp(0.4 * n(N)).astype(np.float32),
    }

def reference(tab_words, tab_scales, offs, pos1, pos2, w1, w4_words, w4_scales, gain, solid, wl, w8_words, w8_scales, fin):
    v = unpack_weight(tab_words, tab_scales, "e4m3")[:, unstriped(offs)]
    w4 = unpack_weight(w4_words, w4_scales, "e2m1")
    w8 = unpack_weight(w8_words, w8_scales, "e4m3")
    e1 = mxq(f64(w1), 0, "e4m3").T @ v
    e2 = w4.T @ v
    h = (e1 + np.maximum(e1, e2)) * f64(gain)[:, None]
    xa = np.abs(h[:, unstriped(pos1)])
    xb = h[:, unstriped(pos2)] * f64(solid)[:, None]
    ya = mxq(f64(wl), 0, "e4m3").T @ mxq(xa, 0, "e4m3")
    yb = w8.T @ mxq(xb, 0, "e4m3")
    return np.minimum(ya, yb) * f64(fin)[:, None]

from contextlib import ExitStack

import concourse.mybir as mybir
from concourse.masks import make_identity

K, H, N, T, S, J = 1024, 1024, 384, 4096, 1024, 512
FLOPS = 2 * (2 * K * H * S + 2 * H * N * J)

F32 = mybir.dt.float32
BF16 = mybir.dt.bfloat16
I32 = mybir.dt.int32
U32 = mybir.dt.uint32
U16 = mybir.dt.uint16
U8 = mybir.dt.uint8
E4M3 = mybir.dt.float8_e4m3fn_x4
E2M1 = mybir.dt.float4_e2m1fn_x4
ALU = mybir.AluOpType
ACT = mybir.ActivationFunctionType

P = 128
PACK = 4
PASS = P * PACK
BANK = 512
NT = N // P
CHUNKS = ((0, 256), (256, 128), (384, 128))


def tile_list_washer_tray_scores_kernel(
    tc, tab_words, tab_scales, offs, pos1, pos2, w1, w4_words, w4_scales, gain, solid, wl, w8_words, w8_scales, fin, out
):
    nc = tc.nc
    with ExitStack() as ctx:
        lists = ctx.enter_context(tc.tile_pool(name="lists", bufs=1))
        keep = ctx.enter_context(tc.tile_pool(name="keep", bufs=1))
        ring = ctx.enter_context(tc.tile_pool(name="ring", bufs=1))
        psum = ctx.enter_context(tc.psum_pool(name="psum", bufs=1))

        def held(name, shape, dtype):
            return keep.tile(shape, dtype, name=name, align_bytes=64)

        def shared(name, tag, bufs, shape, dtype):
            return ring.tile(shape, dtype, name=name, tag=tag, bufs=bufs, align_bytes=64)

        def bank(name, index):
            return psum.tile([P, BANK], F32, name=name, tag="bank%d" % index)

        offs_sb = lists.tile([P, S // 16], U16, name="offs_sb")
        pos1_sb = lists.tile([P, J // 16], U16, name="pos1_sb")
        pos2_sb = lists.tile([P, J // 16], U16, name="pos2_sb")
        nc.sync.dma_start(offs_sb[:], offs)

        def load_table(a):
            words = shared("tab%d" % a, "wide%d" % a, 1, [P, T], I32)
            nc.sync.dma_start(words[:], tab_words[a].rearrange("p t i -> p (t i)").bitcast(I32))
            return words

        def load_rows(name, rows):
            raw = shared(name, "raw", 6, [P, PACK, rows.shape[1]], F32)
            nc.sync.dma_start(raw[:], rows.rearrange("(p j) c -> p j c", j=PACK))
            return raw

        tab_sc = held("tab_sc", [P, 2, T], U8)
        w4_sc = held("w4_sc", [P, 2, H], U8)
        w8_sc = held("w8_sc", [P, 2, N], U8)
        nc.vector.memset(tab_sc[:, 0, :].bitcast(I32), 0)
        nc.gpsimd.memset(tab_sc[:, 1, :].bitcast(I32), 0)
        for plane in (w4_sc, w8_sc):
            nc.vector.memset(plane[:].bitcast(I32), 0)

        def load_scale_rows(plane, rows):
            for q in range(4):
                nc.sync.dma_start(
                    plane[32 * q : 32 * q + 4, :, :].bitcast(I32),
                    rows[:, 4 * q : 4 * q + 4, :].rearrange("a r c -> r a c").bitcast(I32),
                )

        def load_w1(b, a):
            return load_rows("w1_raw%d%d" % (b, a), w1[PASS * a : PASS * (a + 1), PASS * b : PASS * (b + 1)])

        tab = [load_table(0)]
        load_scale_rows(tab_sc, tab_scales)
        w4_raw = held("w4_raw", [P, 2, 2 * H], U8)
        nc.sync.dma_start(w4_raw[:].bitcast(I32), w4_words.rearrange("a p c -> p a c").bitcast(I32))
        w1_raw = {(0, 0): load_w1(0, 0)}
        load_scale_rows(w4_sc, w4_scales)
        w1_raw[0, 1] = load_w1(0, 1)
        tab.append(load_table(1))
        gain_sb = held("gain_sb", [P, 2, PACK], F32)
        solid_sb = held("solid_sb", [P, 2, PACK], F32)
        fin_sb = held("fin_sb", [P, NT], F32)
        nc.gpsimd.dma_start(gain_sb[:], gain.rearrange("(b p t) -> p b t", b=2, t=PACK))
        nc.gpsimd.dma_start(solid_sb[:], solid.rearrange("(b p t) -> p b t", b=2, t=PACK))
        nc.sync.dma_start(pos1_sb[:], pos1)
        nc.sync.dma_start(pos2_sb[:], pos2)
        for a in range(2):
            w1_raw[1, a] = load_w1(1, a)
        wl_raw = [load_rows("wl_raw%d" % a, wl[PASS * a : PASS * (a + 1), :]) for a in range(2)]
        w8_codes = held("w8_codes", [P, 2, N], I32)
        nc.sync.dma_start(w8_codes[:], w8_words.rearrange("a p c i -> p a (c i)").bitcast(I32))
        load_scale_rows(w8_sc, w8_scales)
        with nc.allow_non_contiguous_dma(reason="one factor a partition"):
            nc.sync.dma_start(fin_sb[:], fin.rearrange("(c p) -> p c", p=P))

        picked = {}

        def gather_table(a):
            for h in range(2):
                picked[a, h] = held("picked%d%d" % (a, h), [P, BANK], U32)
                nc.vector.tensor_copy(picked[a, h][:], tab[a][:].bitcast(U32).indirect(offs_sb[:, 32 * h : 32 * (h + 1)]))

        gather_table(0)
        picked_sc = [held("picked_sc%d" % a, [P, S], U8) for a in range(2)]
        for a in range(2):
            nc.vector.tensor_copy(picked_sc[a][:], tab_sc[:, a, :].indirect(offs_sb[:]))
        ident = held("ident", [P, P], F32)
        make_identity(nc, ident[:])

        gain_abs = held("gain_abs", [P, 2 * PACK], F32)
        gain_pos = held("gain_pos", [P, 2 * PACK], F32)
        solid_signed = held("solid_signed", [P, 2 * PACK], F32)
        nc.scalar.activation(gain_abs[:], gain_sb[:].rearrange("p b t -> p (b t)"), ACT.Abs)
        nc.vector.tensor_scalar(gain_pos[:], gain_sb[:].rearrange("p b t -> p (b t)"), 0.0, 2.0, ALU.is_ge, ALU.mult)
        nc.vector.scalar_tensor_tensor(
            solid_signed[:], gain_pos[:], -1.0, solid_sb[:].rearrange("p b t -> p (b t)"), ALU.add, ALU.mult
        )

        w4_dealt = held("w4_dealt", [P, 2, 2 * PASS], U8)
        w4_dealt_sc = held("w4_dealt_sc", [P, 2, PASS], U8)
        nc.vector.tensor_copy(
            w4_dealt[:].bitcast(U16).rearrange("p a (t m) -> p a t m", t=PACK),
            w4_raw[:, :, 0 : 2 * PASS].bitcast(U16).rearrange("p a (m t) -> p a t m", t=PACK),
        )
        nc.vector.tensor_copy(
            w4_dealt_sc[:].rearrange("p a (t m) -> p a t m", t=PACK),
            w4_sc[:, :, 0:PASS].rearrange("p a (m t) -> p a t m", t=PACK),
        )

        w1_codes, w1_sc, w1_bf = {}, {}, {}

        def round_w1(b, a):
            w1_bf[b, a] = shared("w1_bf%d%d" % (b, a), "wbf%d" % a, 1, [P, PACK * PASS], BF16)
            nc.scalar.copy(
                w1_bf[b, a][:].rearrange("p (t m j) -> p m j t", t=PACK, j=PACK),
                w1_raw[b, a][:].rearrange("p j (m t) -> p m j t", t=PACK),
            )

        def quantise(name, rounded):
            width = rounded.shape[1] // PACK
            codes = held(name + "_codes", [P, width], U32)
            scales = held(name + "_sc", [P, width], U8)
            nc.vector.quantize_mx(out=codes[:].bitcast(E4M3), scales=scales[:], in_=rounded)
            return codes, scales

        def quantise_w1(b, a):
            w1_codes[b, a], w1_sc[b, a] = quantise("w1_%d%d" % (b, a), w1_bf[b, a][:])

        for a in range(2):
            round_w1(0, a)
            quantise_w1(0, a)
        gather_table(1)

        e2_sb = [held("e2_sb%d" % t, [P, S], F32) for t in range(PACK)]

        def direct_e2(t):
            for h in range(2):
                acc = bank("e2_%d%d" % (t, h), ((0, 1), (2, 3), (6, 7), (4, 5))[t][h])
                for a in range(2):
                    nc.tensor.matmul_mx(
                        acc[:],
                        lhsT=w4_dealt[:, a, 2 * P * t : 2 * P * (t + 1)].bitcast(E2M1),
                        lhsT_scale=w4_dealt_sc[:, a, P * t : P * (t + 1)],
                        rhs=picked[a, h][:].bitcast(E4M3),
                        rhs_scale=picked_sc[a][:, BANK * h : BANK * (h + 1)],
                        start=(a == 0),
                        stop=(a == 1),
                    )
                nc.scalar.activation(
                    e2_sb[t][:, BANK * h : BANK * (h + 1)], acc[:], ACT.Copy, scale=gain_abs[:, t : t + 1]
                )

        window = [held("window%d" % i, [P, S], F32) for i in range(2 * PACK)]

        def direct_rows(t):
            accs = []
            larger = shared("larger%d" % t, ("larger", "late0", "wbf1", "larger")[t], 1, [P, 2, BANK], F32)
            for h in range(2):
                acc = bank("e1_%d%d" % (t, h), ((6, 7), (4, 5), (6, 7), (3, 7))[t][h])
                for a in range(2):
                    nc.tensor.matmul_mx(
                        acc[:],
                        lhsT=w1_codes[0, a][:, P * t : P * (t + 1)].bitcast(E4M3),
                        lhsT_scale=w1_sc[0, a][:, P * t : P * (t + 1)],
                        rhs=picked[a, h][:].bitcast(E4M3),
                        rhs_scale=picked_sc[a][:, BANK * h : BANK * (h + 1)],
                        start=(a == 0),
                        stop=(a == 1),
                    )
                accs.append(acc)
            for h in range(2):
                nc.vector.scalar_tensor_tensor(
                    larger[:, h, :], accs[h][:], gain_abs[:, t : t + 1], e2_sb[t][:, BANK * h : BANK * (h + 1)],
                    ALU.mult, ALU.max,
                )
            for h in range(2):
                nc.vector.scalar_tensor_tensor(
                    window[t][:, BANK * h : BANK * (h + 1)], accs[h][:], gain_abs[:, t : t + 1], larger[:, h, :],
                    ALU.mult, ALU.add,
                )

        turned = {}

        def turned_rows(s):
            h, i = divmod(s, 4)
            if i == 0:
                turned[h] = shared("turned%d" % h, "wide%d" % h, 1, [P, 2 * 4 * BANK], F32)
            e1_cols = turned[h][:, BANK * i : BANK * (i + 1)]
            max_cols = turned[h][:, BANK * (4 + i) : BANK * (5 + i)]
            acc1 = bank("e1t_%d" % s, (0, 2, 4, 0, 2, 6, 0, 2)[s])
            acc2 = bank("e2t_%d" % s, (1, 3, 5, 1, 3, 7, 1, 6)[s])
            for a in range(2):
                nc.tensor.matmul_mx(
                    acc1[:],
                    lhsT=picked[a, h][:, P * i : P * (i + 1)].bitcast(E4M3),
                    lhsT_scale=picked_sc[a][:, P * s : P * (s + 1)],
                    rhs=w1_codes[1, a][:].bitcast(E4M3),
                    rhs_scale=w1_sc[1, a][:],
                    start=(a == 0),
                    stop=(a == 1),
                )
            for a in range(2):
                nc.tensor.matmul_mx(
                    acc2[:],
                    lhsT=picked[a, h][:, P * i : P * (i + 1)].bitcast(E4M3),
                    lhsT_scale=picked_sc[a][:, P * s : P * (s + 1)],
                    rhs=w4_raw[:, a, 2 * PASS : 4 * PASS].bitcast(E2M1),
                    rhs_scale=w4_sc[:, a, PASS : 2 * PASS],
                    start=(a == 0),
                    stop=(a == 1),
                )
            nc.scalar.copy(e1_cols, acc1[:])
            nc.vector.tensor_tensor(
                max_cols.rearrange("p (t m) -> p t m", t=PACK),
                acc2[:].rearrange("p (m t) -> p t m", t=PACK),
                e1_cols.rearrange("p (t m) -> p t m", t=PACK),
                ALU.max,
            )

        def turn_back(h):
            for t in range(PACK):
                acc = bank("sum_%d%d" % (h, t), ((4, 5, 4, 5), (4, 5, 0, 1))[h][t])
                for i in range(4):
                    for term in range(2):
                        first = BANK * (4 * term + i) + P * t
                        nc.tensor.matmul(
                            acc[:, P * i : P * (i + 1)], turned[h][:, first : first + P], ident[:],
                            is_transpose=True, start=(term == 0), stop=(term == 1),
                        )
                nc.scalar.activation(
                    window[PACK + t][:, BANK * h : BANK * (h + 1)], acc[:], ACT.Copy,
                    scale=gain_abs[:, PACK + t : PACK + t + 1],
                )

        def pick(dst, t, b, offsets):
            nc.vector.tensor_copy(dst, window[PACK * b + t][:].indirect(offsets))

        def woven(tile):
            return tile.rearrange("p (c i t) -> p c t i", i=4, t=PACK)

        def planes(tile):
            return tile[:].rearrange("p t (c i) -> p c t i", i=4)

        def scale_xb(dst, src, t, b):
            nc.scalar.activation(
                dst[:, t, :], src, ACT.Copy, scale=solid_signed[:, PACK * b + t : PACK * b + t + 1]
            )

        ga0 = shared("ga0", "raw", 6, [P, PACK, J], F32)
        gb0 = shared("gb0", "raw", 6, [P, PACK, J], F32)
        xs0 = shared("xs0", "xs", 2, [P, PACK, J], BF16)

        def pick_direct(t):
            pick(gb0[:, t, :], t, 0, pos2_sb[:])
            pick(ga0[:, t, :], t, 0, pos1_sb[:])
            scale_xb(xs0, gb0[:, t, :], t, 0)

        direct_e2(0)
        direct_rows(0)
        direct_e2(1)
        direct_rows(1)
        for a in range(2):
            round_w1(1, a)
        direct_e2(2)
        direct_e2(3)
        pick_direct(0)
        for a in range(2):
            quantise_w1(1, a)
        pick_direct(1)
        for s in range(3):
            turned_rows(s)
        direct_rows(2)
        for s in range(3, 6):
            turned_rows(s)
        turn_back(0)
        pick_direct(2)
        turned_rows(6)
        turned_rows(7)
        direct_rows(3)
        turn_back(1)
        pick_direct(3)

        wl_q = []
        for a in range(2):
            rounded = shared("wl_bf%d" % a, "wbf0" if a == 0 else "wlbf", 1, [P, PACK * N], BF16)
            for part in (slice(0, N // 8), slice(N // 8, N // 4)):
                nc.scalar.copy(woven(rounded[:])[:, part], planes(wl_raw[a])[:, part])
            wl_q.append(quantise("wl_%d" % a, rounded[:]))

        gb1 = [shared("gb1_%d" % u, "late%d" % u, 1, [P, 2, J], F32) for u in range(2)]
        xs1 = shared("xs1", "xs", 2, [P, PACK, J], BF16)
        for t in range(PACK):
            pick(gb1[t // 2][:, t % 2, :], t, 1, pos2_sb[:])
            scale_xb(xs1, gb1[t // 2][:, t % 2, :], t, 1)
        x_bf0 = shared("x_bf0", "wide1", 1, [P, 2 * PACK * J], BF16)
        xb_bf0 = x_bf0[:, 0 : PACK * J]
        xa_bf0 = x_bf0[:, PACK * J : 2 * PACK * J]
        halves = (slice(0, J // 8), slice(J // 8, J // 4))
        for part in halves:
            nc.scalar.copy(woven(xb_bf0)[:, part], planes(xs0)[:, part])
        for part in halves:
            nc.scalar.activation(woven(xa_bf0)[:, part], planes(ga0)[:, part], ACT.Abs)
        xb_bf1 = held("xb_bf1", [P, PACK * J], BF16)
        nc.vector.tensor_copy(woven(xb_bf1[:]), planes(xs1))
        xb_q = [quantise("xb_0", xb_bf0)]

        xa_bf1 = []

        def pick_chunk(c):
            first, width = CHUNKS[c]
            ga1 = shared("ga1_%d" % c, "late%d" % (c % 2), 1, [P, PACK, width], F32)
            for t in range(PACK):
                pick(ga1[:, t, :], t, 1, pos1_sb[:, first // 16 : (first + width) // 16])
            xa_bf1.append(held("xa_bf1_%d" % c, [P, PACK * width], BF16))
            nc.scalar.activation(woven(xa_bf1[c][:]), planes(ga1), ACT.Abs)

        pick_chunk(0)
        xb_q.append(quantise("xb_1", xb_bf1[:]))
        xa_q0 = quantise("xa_0", xa_bf0)
        yb_sb = shared("yb_sb", "raw", 6, [P, NT, J], F32)
        for n in range(NT):
            acc = bank("yb_%d" % n, n)
            for a in range(2):
                nc.tensor.matmul_mx(
                    acc[:],
                    lhsT=w8_codes[:, a, P * n : P * (n + 1)].bitcast(E4M3),
                    lhsT_scale=w8_sc[:, a, P * n : P * (n + 1)],
                    rhs=xb_q[a][0][:].bitcast(E4M3),
                    rhs_scale=xb_q[a][1][:],
                    start=(a == 0),
                    stop=(a == 1),
                )
            nc.scalar.copy(yb_sb[:, n, :], acc[:])

        out_rows = out.rearrange("(n p) j -> p n j", p=P)
        ya_banks = ((3, 4), (5,), (6,))
        ya_acc = {}

        def multiply_chunk(c):
            first, width = CHUNKS[c]
            xa_q1 = quantise("xa_1_%d" % c, xa_bf1[c][:])
            per_bank = min(NT, BANK // width)
            ya_acc[c] = []
            for index, n0 in zip(ya_banks[c], range(0, NT, per_bank)):
                tiles = range(n0, min(NT, n0 + per_bank))
                acc = bank("ya_%d_%d" % (c, n0), index)
                for a in range(2):
                    for n in tiles:
                        cols = slice(first, first + width) if a == 0 else slice(0, width)
                        codes, scales = xa_q0 if a == 0 else xa_q1
                        nc.tensor.matmul_mx(
                            acc[:, width * (n - n0) : width * (n - n0 + 1)],
                            lhsT=wl_q[a][0][:, P * n : P * (n + 1)].bitcast(E4M3),
                            lhsT_scale=wl_q[a][1][:, P * n : P * (n + 1)],
                            rhs=codes[:, cols].bitcast(E4M3),
                            rhs_scale=scales[:, cols],
                            start=(a == 0 and n == tiles[0]),
                            stop=(a == 1 and n == tiles[-1]),
                        )
                ya_acc[c].append((acc, n0, len(tiles)))

        def finish_chunk(c):
            first, width = CHUNKS[c]
            lower = held("lower%d" % c, [P, NT, width], F32)
            for acc, n0, count in ya_acc[c]:
                nc.vector.tensor_tensor(
                    lower[:, n0 : n0 + count, :],
                    acc[:, 0 : width * count].rearrange("p (n j) -> p n j", n=count),
                    yb_sb[:, n0 : n0 + count, first : first + width],
                    ALU.min,
                )
            if c == 0:
                for n in range(NT):
                    nc.scalar.activation(lower[:, n, :], lower[:, n, :], ACT.Copy, scale=fin_sb[:, n : n + 1])
            else:
                nc.vector.tensor_tensor(
                    lower[:], lower[:], fin_sb[:].unsqueeze(2).to_broadcast([P, NT, width]), ALU.mult
                )
            nc.sync.dma_start(out_rows[:, :, first : first + width], lower[:])

        pick_chunk(1)
        multiply_chunk(0)
        pick_chunk(2)
        multiply_chunk(1)
        finish_chunk(0)
        multiply_chunk(2)
        finish_chunk(1)
        finish_chunk(2)
